import numpy as np
import ml_dtypes


def mxq(x, axis, fmt="e4m3"):
    dtype, down = {"e4m3": (ml_dtypes.float8_e4m3fn, 7), "e5m2": (ml_dtypes.float8_e5m2, 14)}[fmt]
    v = np.moveaxis(np.asarray(x, np.float32).astype(ml_dtypes.bfloat16).astype(np.float64), axis, -1)
    blocks = v.reshape(v.shape[:-1] + (-1, 32))
    amax = np.abs(blocks).max(-1, keepdims=True)
    byte = np.maximum(np.where(amax > 0, np.frexp(amax)[1] - 1 + 127, 0) - down, 1)
    scale = np.exp2(byte - 127.0)
    codes = (blocks / scale).astype(np.float32).astype(dtype).astype(np.float64)
    return np.moveaxis((codes * scale).reshape(v.shape), -1, axis)


WIDE = False


def mx_kscale(k):
    if not WIDE:
        return np.ones(k)
    levels = np.array([30, -30])
    if k % 512:
        return np.exp2(np.random.permutation(np.resize(levels, k // 32))).repeat(32)
    a = np.empty((k // 512, 16))
    for p in range(k // 512):
        a[p, :8] = np.random.permutation(np.resize(levels, 8))
        for g in range(8):
            far = levels[np.abs(levels - a[p, g]) >= 10]
            a[p, g + 8] = far[np.random.randint(len(far))]
    return np.exp2(a.ravel()).repeat(32)


def f64(x):
    return np.asarray(x).astype(np.float64)


def striped(idx):
    return np.tile(idx.reshape(-1, 16).T, (8, 1)).astype(np.uint16)


def unstriped(offs):
    return offs[:16].T.reshape(-1).astype(np.int64)


K, T, E, C, N = 512, 2048, 4, 512, 512


def by_expert(wq, xq):
    return np.concatenate([wq[e].T @ xq[:, e * C:(e + 1) * C] for e in range(E)], axis=1)


def setup_inputs():
    n = np.random.standard_normal
    s = mx_kscale(N)[:, None]
    return {
        "dyT": (n((N, T)) * s).astype(np.float32),
        "w": (n((E + 1, N, K)) / np.sqrt(N) / s[None]).astype(np.float32),
        "gate": np.tile(np.random.uniform(0.2, 1.0, E * C), (N, 1)).astype(np.float32),
        "offs": striped(np.random.permutation(T)[:E * C]),
    }


def reference(dyT, w, gate, offs):
    idx = unstriped(offs)
    gq = mxq(f64(gate) * f64(dyT)[:, idx], 0, "e5m2")
    wq = mxq(f64(w), 1, "e4m3")
    ds = wq[E].T @ mxq(f64(dyT), 0, "e5m2")
    dx = by_expert(wq, gq)
    ds[:, idx] += dx
    return ds

@@ -1,0 +1,169 @@
+from contextlib import ExitStack
+
+import concourse.mybir as mybir
+
+K, T, E, C, N = 512, 2048, 4, 512, 512
+FLOPS = 2 * 2 * N * K * T
+BYTES = 4 * (N * T + (E + 1) * N * K + T + K * T) + 2 * T
+
+F32 = mybir.dt.float32
+BF16 = mybir.dt.bfloat16
+U32 = mybir.dt.uint32
+U16 = mybir.dt.uint16
+U8 = mybir.dt.uint8
+E4M3 = mybir.dt.float8_e4m3fn_x4
+E5M2 = mybir.dt.float8_e5m2_x4
+MULT = mybir.AluOpType.mult
+COPY = mybir.ActivationFunctionType.Copy
+
+P = 128
+PACK = 4
+SHARED = E
+KB = K // P
+HALF = K // 2
+PER_COL = 16
+SCALAR_SCATTER = 256
+
+
+def planes_view(t):
+    return t.rearrange("p j (c i) -> p c j i", i=4)
+
+
+def woven_view(t):
+    return t.rearrange("p (c i j) -> p c j i", i=4, j=PACK)
+
+
+def tile_moe_bds_lin_none_kernel(tc, dyT, w, gate, offs, out):
+    nc = tc.nc
+    with ExitStack() as ctx:
+        keep = ctx.enter_context(tc.tile_pool(name="keep", bufs=1))
+        stage = ctx.enter_context(tc.tile_pool(name="stage", bufs=2))
+        psum = ctx.enter_context(tc.psum_pool(name="psum", bufs=8))
+
+        offsets = keep.tile([P, T // PER_COL], U16, name="offsets")
+        nc.sync.dma_start(offsets[:], offs)
+
+        def slots(a, n):
+            return offsets[:, a // PER_COL : (a + n) // PER_COL]
+
+        dy_rows = dyT.rearrange("(p j) t -> p j t", j=PACK)
+        dy = [keep.tile([P, T], F32, name="dy%d" % j) for j in range(PACK)]
+        for j in range(PACK):
+            nc.sync.dma_start(dy[j][:], dy_rows[:, j, :])
+
+        gates = [keep.tile([P, C], F32, name="gate%d" % e) for e in range(E)]
+        w_raw = {}
+
+        def load_gate(e):
+            nc.sync.dma_start(gates[e][:], gate[0:P, e * C : (e + 1) * C])
+
+        def load_w(m, h):
+            w_raw[m, h] = keep.tile([P, PACK, HALF], F32, name="w%d_%d" % (m, h))
+            rows = w[m].rearrange("(p j) k -> p j k", j=PACK)
+            nc.sync.dma_start(w_raw[m, h][:], rows[:, :, h * HALF : (h + 1) * HALF])
+
+        load_gate(0)
+        for h in range(2):
+            load_w(SHARED, h)
+            load_w(0, h)
+        for e in range(1, E):
+            load_gate(e)
+            load_w(e, 0)
+            load_w(e, 1)
+
+        picked = [keep.tile([P, PACK, C], F32, name="picked%d" % e) for e in range(E)]
+
+        def gather(e, j, on_vector):
+            src = dy[j][:].indirect(slots(e * C, C))
+            if on_vector:
+                nc.vector.tensor_copy(picked[e][:, j, :], src)
+            else:
+                nc.scalar.activation(picked[e][:, j, :], src, COPY)
+
+        for j in range(PACK):
+            for e in range(E):
+                gather(e, j, e == 0 or (e == 1 and j < PACK - 1))
+
+        w_codes = [keep.tile([P, K], U32, name="wc%d" % m, align_bytes=64) for m in range(E + 1)]
+        w_scales = [keep.tile([P, K], U8, name="ws%d" % m, align_bytes=64) for m in range(E + 1)]
+        a_codes = [keep.tile([P, 2 * C], U32, name="ac%d" % e, align_bytes=64) for e in range(E)]
+        a_scales = [keep.tile([P, 2 * C], U8, name="as%d" % e, align_bytes=64) for e in range(E)]
+        sums = [keep.tile([P, T], F32, name="sums%d" % b) for b in range(KB)]
+        result = [keep.tile([P, T], F32, name="result%d" % b) for b in range(KB)]
+
+        def weave_w(m, h, on_vector):
+            wb = stage.tile([P, PACK * HALF], BF16, name="wb", bufs=4, align_bytes=64)
+            if on_vector:
+                nc.vector.tensor_copy(woven_view(wb[:]), planes_view(w_raw[m, h][:]))
+            else:
+                nc.scalar.copy(woven_view(wb[:]), planes_view(w_raw[m, h][:]))
+            return wb
+
+        def quantize_w(m, h, wb):
+            cols = slice(h * HALF, (h + 1) * HALF)
+            nc.vector.quantize_mx(w_codes[m][:, cols].bitcast(E4M3), w_scales[m][:, cols], wb[:])
+
+        def weave_a(e):
+            ab = stage.tile([P, 2 * PACK * C], BF16, name="ab", align_bytes=64)
+            g = gates[e][:].rearrange("p (c i) -> p c i", i=4).unsqueeze(2).to_broadcast([P, C // 4, PACK, 4])
+            nc.vector.tensor_tensor(woven_view(ab[:, 0 : PACK * C]), planes_view(picked[e][:]), g, MULT)
+            nc.vector.tensor_copy(woven_view(ab[:, PACK * C : 2 * PACK * C]), planes_view(picked[e][:]))
+            return ab
+
+        def quantize_a(e, ab):
+            nc.vector.quantize_mx(a_codes[e][:].bitcast(E5M2), a_scales[e][:], ab[:])
+
+        def products(e, b, on_vector):
+            acc = psum.tile([P, C], F32, name="acc")
+            kc = slice(b * P, (b + 1) * P)
+            for s, m in ((0, e), (1, SHARED)):
+                cols = slice(s * C, (s + 1) * C)
+                nc.tensor.matmul_mx(
+                    acc[:],
+                    lhsT=w_codes[m][:, kc].bitcast(E4M3),
+                    lhsT_scale=w_scales[m][:, kc],
+                    rhs=a_codes[e][:, cols].bitcast(E5M2),
+                    rhs_scale=a_scales[e][:, cols],
+                    start=(s == 0),
+                    stop=(s == 1),
+                )
+            if on_vector:
+                nc.vector.tensor_copy(sums[b][:, e * C : (e + 1) * C], acc[:])
+            else:
+                nc.scalar.copy(sums[b][:, e * C : (e + 1) * C], acc[:])
+
+        def scatter_scalar(b, a, n):
+            for x in range(a, a + n, SCALAR_SCATTER):
+                nc.scalar.activation(
+                    result[b][:].indirect(slots(x, SCALAR_SCATTER)), sums[b][:, x : x + SCALAR_SCATTER], COPY
+                )
+
+        def scatter_vector(b, a, n):
+            nc.vector.tensor_copy(result[b][:].indirect(slots(a, n)), sums[b][:, a : a + n])
+
+        ab = weave_a(0)
+        first = [(m, h, weave_w(m, h, False)) for h in range(2) for m in (SHARED, 0)]
+        quantize_a(0, ab)
+        for m, h, wb in first:
+            quantize_w(m, h, wb)
+
+        for e in range(E):
+            for b in range(KB):
+                products(e, b, b == 0 or (b == 3 and e >= 2))
+            if e + 1 < E:
+                ab = weave_a(e + 1)
+                wbs = [weave_w(e + 1, h, True) for h in range(2)]
+                quantize_a(e + 1, ab)
+                for h in range(2):
+                    quantize_w(e + 1, h, wbs[h])
+            if e < 2:
+                scatter_scalar(3, e * C, C)
+            scatter_scalar(1, e * C, C)
+            scatter_scalar(2, e * C, C)
+        for e in range(E):
+            scatter_vector(0, e * C, C)
+        nc.sync.dma_start(out[0:P, :], result[0][:])
+        nc.sync.dma_start(out[P : 2 * P, :], result[1][:])
+        scatter_vector(3, 2 * C, 2 * C)
+        nc.scalar.dma_start(out[2 * P : 3 * P, :], result[2][:])
+        nc.sync.dma_start(out[3 * P : 4 * P, :], result[3][:])

@@ -47,81 +47,100 @@ def tile_moe_bds_lin_none_kernel(tc, dyT, w, gate, offs, out):
             return offsets[:, a // PER_COL : (a + n) // PER_COL]
 
         dy_rows = dyT.rearrange("(p j) t -> p j t", j=PACK)
-        dy = [keep.tile([P, T], F32, name="dy%d" % j) for j in range(PACK)]
-        for j in range(PACK):
-            nc.sync.dma_start(dy[j][:], dy_rows[:, j, :])
-
+        dy = [keep.tile([P, T], F32, name="dy%d" % j, tag="row%d" % j) for j in range(PACK)]
         gates = [keep.tile([P, C], F32, name="gate%d" % e) for e in range(E)]
         w_raw = {}
+
+        def load_dy(j):
+            nc.sync.dma_start(dy[j][:], dy_rows[:, j, :])
 
         def load_gate(e):
             nc.sync.dma_start(gates[e][:], gate[0:P, e * C : (e + 1) * C])
 
         def load_w(m, h):
-            w_raw[m, h] = keep.tile([P, PACK, HALF], F32, name="w%d_%d" % (m, h))
+            t = keep.tile([P, PACK, HALF], F32, name="w%d_%d" % (m, h))
             rows = w[m].rearrange("(p j) k -> p j k", j=PACK)
-            nc.sync.dma_start(w_raw[m, h][:], rows[:, :, h * HALF : (h + 1) * HALF])
+            nc.sync.dma_start(t[:], rows[:, :, h * HALF : (h + 1) * HALF])
+            w_raw[m, h] = t[:]
 
+        def load_w_whole(m):
+            t = keep.tile([P, PACK, K], F32, name="w%d" % m)
+            nc.sync.dma_start(t[:], w[m].rearrange("(p j) k -> p j k", j=PACK))
+            w_raw[m, None] = t[:]
+
+        for j in range(PACK):
+            load_dy(j)
         load_gate(0)
         for h in range(2):
             load_w(SHARED, h)
             load_w(0, h)
         for e in range(1, E):
             load_gate(e)
-            load_w(e, 0)
-            load_w(e, 1)
+            load_w_whole(e)
 
-        picked = [keep.tile([P, PACK, C], F32, name="picked%d" % e) for e in range(E)]
+        pairs = [keep.tile([P, PACK, 2 * C], F32, name="picked%d" % u) for u in range(E // 2)]
+        picked = [pairs[e // 2][:, :, (e % 2) * C : (e % 2 + 1) * C] for e in range(E)]
 
-        def gather(e, j, on_vector):
-            src = dy[j][:].indirect(slots(e * C, C))
+        def gather(a, n, j, on_vector):
+            src = dy[j][:].indirect(slots(a, n))
+            u, x = divmod(a, 2 * C)
+            dst = pairs[u][:, j, x : x + n]
             if on_vector:
-                nc.vector.tensor_copy(picked[e][:, j, :], src)
+                nc.vector.tensor_copy(dst, src)
             else:
-                nc.scalar.activation(picked[e][:, j, :], src, COPY)
+                nc.scalar.activation(dst, src, COPY)
 
-        for j in range(PACK):
-            for e in range(E):
-                gather(e, j, e == 0 or (e == 1 and j < PACK - 1))
-
-        w_codes = [keep.tile([P, K], U32, name="wc%d" % m, align_bytes=64) for m in range(E + 1)]
-        w_scales = [keep.tile([P, K], U8, name="ws%d" % m, align_bytes=64) for m in range(E + 1)]
+        w_codes = {}
+        w_scales = {}
         a_codes = [keep.tile([P, 2 * C], U32, name="ac%d" % e, align_bytes=64) for e in range(E)]
         a_scales = [keep.tile([P, 2 * C], U8, name="as%d" % e, align_bytes=64) for e in range(E)]
-        sums = [keep.tile([P, T], F32, name="sums%d" % b) for b in range(KB)]
         result = [keep.tile([P, T], F32, name="result%d" % b) for b in range(KB)]
 
         def weave_w(m, h, on_vector):
-            wb = stage.tile([P, PACK * HALF], BF16, name="wb", bufs=4, align_bytes=64)
-            if on_vector:
-                nc.vector.tensor_copy(woven_view(wb[:]), planes_view(w_raw[m, h][:]))
+            if h is None:
+                wb = stage.tile([P, PACK * K], BF16, name="wb_whole", bufs=2, align_bytes=64)
             else:
-                nc.scalar.copy(woven_view(wb[:]), planes_view(w_raw[m, h][:]))
+                wb = stage.tile([P, PACK * HALF], BF16, name="wb", bufs=4, align_bytes=64)
+            if on_vector:
+                nc.vector.tensor_copy(woven_view(wb[:]), planes_view(w_raw[m, h]))
+            else:
+                nc.scalar.copy(woven_view(wb[:]), planes_view(w_raw[m, h]))
             return wb
 
         def quantize_w(m, h, wb):
-            cols = slice(h * HALF, (h + 1) * HALF)
-            nc.vector.quantize_mx(w_codes[m][:, cols].bitcast(E4M3), w_scales[m][:, cols], wb[:])
+            width = K if h is None else HALF
+            codes = keep.tile([P, width], U32, name="wc%d_%s" % (m, h), align_bytes=64)
+            scales = keep.tile([P, width], U8, name="ws%d_%s" % (m, h), align_bytes=64)
+            nc.vector.quantize_mx(codes[:].bitcast(E4M3), scales[:], wb[:])
+            for x in range(width // P):
+                b = x + 2 * (h or 0)
+                w_codes[m, b] = codes[:, x * P : (x + 1) * P]
+                w_scales[m, b] = scales[:, x * P : (x + 1) * P]
 
-        def weave_a(e):
-            ab = stage.tile([P, 2 * PACK * C], BF16, name="ab", align_bytes=64)
+        def new_a():
+            return stage.tile([P, 2 * PACK * C], BF16, name="ab", align_bytes=64)
+
+        def weave_gated(e, ab):
             g = gates[e][:].rearrange("p (c i) -> p c i", i=4).unsqueeze(2).to_broadcast([P, C // 4, PACK, 4])
-            nc.vector.tensor_tensor(woven_view(ab[:, 0 : PACK * C]), planes_view(picked[e][:]), g, MULT)
-            nc.vector.tensor_copy(woven_view(ab[:, PACK * C : 2 * PACK * C]), planes_view(picked[e][:]))
-            return ab
+            nc.vector.tensor_tensor(woven_view(ab[:, 0 : PACK * C]), planes_view(picked[e]), g, MULT)
+
+        def weave_plain(e, ab, on_vector):
+            if on_vector:
+                nc.vector.tensor_copy(woven_view(ab[:, PACK * C : 2 * PACK * C]), planes_view(picked[e]))
+            else:
+                nc.scalar.copy(woven_view(ab[:, PACK * C : 2 * PACK * C]), planes_view(picked[e]))
 
         def quantize_a(e, ab):
             nc.vector.quantize_mx(a_codes[e][:].bitcast(E5M2), a_scales[e][:], ab[:])
 
         def products(e, b, on_vector):
             acc = psum.tile([P, C], F32, name="acc")
-            kc = slice(b * P, (b + 1) * P)
             for s, m in ((0, e), (1, SHARED)):
                 cols = slice(s * C, (s + 1) * C)
                 nc.tensor.matmul_mx(
                     acc[:],
-                    lhsT=w_codes[m][:, kc].bitcast(E4M3),
-                    lhsT_scale=w_scales[m][:, kc],
+                    lhsT=w_codes[m, b].bitcast(E4M3),
+                    lhsT_scale=w_scales[m, b],
                     rhs=a_codes[e][:, cols].bitcast(E5M2),
                     rhs_scale=a_scales[e][:, cols],
                     start=(s == 0),
@@ -141,29 +160,52 @@ def tile_moe_bds_lin_none_kernel(tc, dyT, w, gate, offs, out):
         def scatter_vector(b, a, n):
             nc.vector.tensor_copy(result[b][:].indirect(slots(a, n)), sums[b][:, a : a + n])
 
-        ab = weave_a(0)
-        first = [(m, h, weave_w(m, h, False)) for h in range(2) for m in (SHARED, 0)]
+        for j in range(PACK - 1):
+            gather(0, 2 * C, j, True)
+            gather(2 * C, 2 * C, j, False)
+        gather(0, C, PACK - 1, True)
+        gather(C, C, PACK - 1, False)
+        ab = new_a()
+        weave_plain(0, ab, False)
+        gather(2 * C, 2 * C, PACK - 1, False)
+        sums = [keep.tile([P, T], F32, name="sums%d" % b, tag="row%d" % b) for b in range(KB)]
+        weave_gated(0, ab)
+        early = [(m, 0, weave_w(m, 0, True)) for m in (SHARED, 0)]
+        late = [(m, 1, weave_w(m, 1, False)) for m in (SHARED, 0)]
         quantize_a(0, ab)
-        for m, h, wb in first:
+        for m, h, wb in early:
             quantize_w(m, h, wb)
 
         for e in range(E):
-            for b in range(KB):
-                products(e, b, b == 0 or (b == 3 and e >= 2))
+            if e == 0:
+                products(0, 0, False)
+                products(0, 1, False)
+            else:
+                for b in (2, 0, 1, 3):
+                    products(e, b, b == 2 or (b == 3 and e >= 2))
             if e + 1 < E:
-                ab = weave_a(e + 1)
-                wbs = [weave_w(e + 1, h, True) for h in range(2)]
+                ab = new_a()
+                weave_gated(e + 1, ab)
+                if e == 0:
+                    for m, h, wb in late:
+                        quantize_w(m, h, wb)
+                weave_plain(e + 1, ab, True)
+                wb = weave_w(e + 1, None, True)
+                if e == 0:
+                    products(0, 2, True)
                 quantize_a(e + 1, ab)
-                for h in range(2):
-                    quantize_w(e + 1, h, wbs[h])
+                quantize_w(e + 1, None, wb)
+            if e == E - 2:
+                scatter_vector(2, 0, (E - 1) * C)
+            scatter_scalar(0, e * C, C)
+            scatter_scalar(1, e * C, C)
+            if e == 0:
+                products(0, 3, False)
             if e < 2:
                 scatter_scalar(3, e * C, C)
-            scatter_scalar(1, e * C, C)
-            scatter_scalar(2, e * C, C)
-        for e in range(E):
-            scatter_vector(0, e * C, C)
+        scatter_vector(2, (E - 1) * C, C)
+        nc.sync.dma_start(out[2 * P : 3 * P, :], result[2][:])
         nc.sync.dma_start(out[0:P, :], result[0][:])
-        nc.sync.dma_start(out[P : 2 * P, :], result[1][:])
         scatter_vector(3, 2 * C, 2 * C)
-        nc.scalar.dma_start(out[2 * P : 3 * P, :], result[2][:])
+        nc.scalar.dma_start(out[P : 2 * P, :], result[1][:])
         nc.sync.dma_start(out[3 * P : 4 * P, :], result[3][:])

@@ -14,6 +14,7 @@ U8 = mybir.dt.uint8
 E4M3 = mybir.dt.float8_e4m3fn_x4
 E5M2 = mybir.dt.float8_e5m2_x4
 MULT = mybir.AluOpType.mult
+ADD = mybir.AluOpType.add
 COPY = mybir.ActivationFunctionType.Copy
 
 P = 128
@@ -64,7 +65,7 @@ def tile_moe_bds_lin_none_kernel(tc, dyT, w, gate, offs, out):
             w_raw[m, h] = t[:]
 
         def load_w_whole(m):
-            t = keep.tile([P, PACK, K], F32, name="w%d" % m)
+            t = keep.tile([P, PACK, K], F32, name="w%d" % m, tag="w%d" % m, align_bytes=64)
             nc.sync.dma_start(t[:], w[m].rearrange("(p j) k -> p j k", j=PACK))
             w_raw[m, None] = t[:]
 
@@ -96,46 +97,52 @@ def tile_moe_bds_lin_none_kernel(tc, dyT, w, gate, offs, out):
         a_scales = [keep.tile([P, 2 * C], U8, name="as%d" % e, align_bytes=64) for e in range(E)]
         result = [keep.tile([P, T], F32, name="result%d" % b) for b in range(KB)]
 
-        def weave_w(m, h, on_vector):
-            if h is None:
-                wb = stage.tile([P, PACK * K], BF16, name="wb_whole", bufs=2, align_bytes=64)
+        def weave(engine, dst, src):
+            if engine == "vector":
+                nc.vector.tensor_copy(woven_view(dst), planes_view(src))
+            elif engine == "scalar":
+                nc.scalar.copy(woven_view(dst), planes_view(src))
             else:
-                wb = stage.tile([P, PACK * HALF], BF16, name="wb", bufs=4, align_bytes=64)
-            if on_vector:
-                nc.vector.tensor_copy(woven_view(wb[:]), planes_view(w_raw[m, h]))
-            else:
-                nc.scalar.copy(woven_view(wb[:]), planes_view(w_raw[m, h]))
-            return wb
+                nc.gpsimd.tensor_scalar(
+                    dst.rearrange("p (c j) -> p c j", j=PACK), src.rearrange("p j c -> p c j"), 1.0, 0.0, MULT, ADD
+                )
 
-        def quantize_w(m, h, wb):
-            width = K if h is None else HALF
-            codes = keep.tile([P, width], U32, name="wc%d_%s" % (m, h), align_bytes=64)
-            scales = keep.tile([P, width], U8, name="ws%d_%s" % (m, h), align_bytes=64)
-            nc.vector.quantize_mx(codes[:].bitcast(E4M3), scales[:], wb[:])
-            for x in range(width // P):
-                b = x + 2 * (h or 0)
-                w_codes[m, b] = codes[:, x * P : (x + 1) * P]
-                w_scales[m, b] = scales[:, x * P : (x + 1) * P]
+        def weave_w(m, h, engine):
+            wb = stage.tile([P, PACK * HALF], BF16, name="wb", bufs=4, align_bytes=64)
+            weave(engine, wb[:], w_raw[m, h])
+            return wb[:]
 
-        def new_a():
-            return stage.tile([P, 2 * PACK * C], BF16, name="ab", align_bytes=64)
+        def w_blocks(m, first, count):
+            return w_raw[m, None][:, :, first * P : (first + count) * P]
 
-        def weave_gated(e, ab):
+        def quantize_w(m, first, count, src):
+            codes = keep.tile([P, count * P], U32, name="wc%d_%d" % (m, first), align_bytes=64)
+            scales = keep.tile([P, count * P], U8, name="ws%d_%d" % (m, first), align_bytes=64)
+            nc.vector.quantize_mx(codes[:].bitcast(E4M3), scales[:], src)
+            for x in range(count):
+                w_codes[m, first + x] = codes[:, x * P : (x + 1) * P]
+                w_scales[m, first + x] = scales[:, x * P : (x + 1) * P]
+
+        def weave_gated(e, tag):
+            gb = keep.tile([P, PACK * C], BF16, name="gated%d" % e, tag=tag, align_bytes=64)
             g = gates[e][:].rearrange("p (c i) -> p c i", i=4).unsqueeze(2).to_broadcast([P, C // 4, PACK, 4])
-            nc.vector.tensor_tensor(woven_view(ab[:, 0 : PACK * C]), planes_view(picked[e]), g, MULT)
+            nc.vector.tensor_tensor(woven_view(gb[:]), planes_view(picked[e]), g, MULT)
+            return gb[:]
 
-        def weave_plain(e, ab, on_vector):
-            if on_vector:
-                nc.vector.tensor_copy(woven_view(ab[:, PACK * C : 2 * PACK * C]), planes_view(picked[e]))
-            else:
-                nc.scalar.copy(woven_view(ab[:, PACK * C : 2 * PACK * C]), planes_view(picked[e]))
+        def weave_plain(e, engine):
+            db = keep.tile([P, PACK * C], BF16, name="plain%d" % e, tag="plain", align_bytes=64)
+            weave(engine, db[:], picked[e])
+            return db[:]
 
-        def quantize_a(e, ab):
-            nc.vector.quantize_mx(a_codes[e][:].bitcast(E5M2), a_scales[e][:], ab[:])
+        def quantize_a(e, s, src):
+            cols = slice(s * C, (s + 1) * C)
+            nc.vector.quantize_mx(a_codes[e][:, cols].bitcast(E5M2), a_scales[e][:, cols], src)
 
-        def products(e, b, on_vector):
+        banks = {}
+
+        def multiply(e, b):
             acc = psum.tile([P, C], F32, name="acc")
-            for s, m in ((0, e), (1, SHARED)):
+            for s, m in ((1, SHARED), (0, e)):
                 cols = slice(s * C, (s + 1) * C)
                 nc.tensor.matmul_mx(
                     acc[:],
@@ -143,13 +150,19 @@ def tile_moe_bds_lin_none_kernel(tc, dyT, w, gate, offs, out):
                     lhsT_scale=w_scales[m, b],
                     rhs=a_codes[e][:, cols].bitcast(E5M2),
                     rhs_scale=a_scales[e][:, cols],
-                    start=(s == 0),
-                    stop=(s == 1),
+                    start=(s == 1),
+                    stop=(s == 0),
                 )
+            banks[e, b] = acc
+
+        def empty(e, b, on_vector):
             if on_vector:
-                nc.vector.tensor_copy(sums[b][:, e * C : (e + 1) * C], acc[:])
+                nc.vector.tensor_copy(sums[b][:, e * C : (e + 1) * C], banks[e, b][:])
             else:
-                nc.scalar.copy(sums[b][:, e * C : (e + 1) * C], acc[:])
+                nc.scalar.copy(sums[b][:, e * C : (e + 1) * C], banks[e, b][:])
+
+        def store(b, queue):
+            queue.dma_start(out[b * P : (b + 1) * P, :], result[b][:])
 
         def scatter_scalar(b, a, n):
             for x in range(a, a + n, SCALAR_SCATTER):
@@ -165,47 +178,100 @@ def tile_moe_bds_lin_none_kernel(tc, dyT, w, gate, offs, out):
             gather(2 * C, 2 * C, j, False)
         gather(0, C, PACK - 1, True)
         gather(C, C, PACK - 1, False)
-        ab = new_a()
-        weave_plain(0, ab, False)
+        db = weave_plain(0, "scalar")
         gather(2 * C, 2 * C, PACK - 1, False)
         sums = [keep.tile([P, T], F32, name="sums%d" % b, tag="row%d" % b) for b in range(KB)]
-        weave_gated(0, ab)
-        early = [(m, 0, weave_w(m, 0, True)) for m in (SHARED, 0)]
-        late = [(m, 1, weave_w(m, 1, False)) for m in (SHARED, 0)]
-        quantize_a(0, ab)
+        gb = weave_gated(0, "gated0")
+        early = [(m, 0, weave_w(m, 0, "vector")) for m in (SHARED, 0)]
+        late = [(m, 1, weave_w(m, 1, "scalar")) for m in (SHARED, 0)]
+        quantize_a(0, 0, gb)
+        quantize_a(0, 1, db)
         for m, h, wb in early:
-            quantize_w(m, h, wb)
+            quantize_w(m, 2 * h, 2, wb)
+        multiply(0, 0)
+        multiply(0, 1)
 
-        for e in range(E):
-            if e == 0:
-                products(0, 0, False)
-                products(0, 1, False)
-            else:
-                for b in (2, 0, 1, 3):
-                    products(e, b, b == 2 or (b == 3 and e >= 2))
-            if e + 1 < E:
-                ab = new_a()
-                weave_gated(e + 1, ab)
-                if e == 0:
-                    for m, h, wb in late:
-                        quantize_w(m, h, wb)
-                weave_plain(e + 1, ab, True)
-                wb = weave_w(e + 1, None, True)
-                if e == 0:
-                    products(0, 2, True)
-                quantize_a(e + 1, ab)
-                quantize_w(e + 1, None, wb)
-            if e == E - 2:
-                scatter_vector(2, 0, (E - 1) * C)
-            scatter_scalar(0, e * C, C)
-            scatter_scalar(1, e * C, C)
-            if e == 0:
-                products(0, 3, False)
-            if e < 2:
-                scatter_scalar(3, e * C, C)
-        scatter_vector(2, (E - 1) * C, C)
-        nc.sync.dma_start(out[2 * P : 3 * P, :], result[2][:])
-        nc.sync.dma_start(out[0:P, :], result[0][:])
+        gb = weave_gated(1, "gated1")
+        for m, h, wb in late:
+            quantize_w(m, 2 * h, 2, wb)
+        multiply(0, 2)
+        multiply(0, 3)
+        db = weave_plain(1, "vector")
+        w1 = keep.tile([P, 3 * PACK * P], BF16, name="w1_woven", align_bytes=64)
+        weave("vector", w1[:], w_blocks(1, 0, 3))
+        quantize_a(1, 1, db)
+        quantize_w(1, 0, 3, w1[:])
+        quantize_a(1, 0, gb)
+
+        first = keep.tile([P, 3 * PACK * C], BF16, name="first", tag="gated1", align_bytes=64)
+        d2, d3 = first[:, 0:2048], first[:, 2048:4096]
+        w2, w1_last = first[:, 4096:5632], first[:, 5632:6144]
+        weave("gpsimd", d2, picked[2])
+        weave("gpsimd", w2, w_blocks(2, 0, 3))
+        weave("gpsimd", d3, picked[3])
+        weave("gpsimd", w1_last, w_blocks(1, 3, 1))
+        empty(0, 0, False)
+        empty(0, 1, False)
+        scatter_scalar(0, 0, C)
+        scatter_scalar(1, 0, C)
+        empty(0, 3, False)
+        scatter_scalar(3, 0, C)
+        for b in (2, 0, 1):
+            multiply(1, b)
+        for e in range(2):
+            empty(e, 2, True)
+            scatter_vector(2, e * C, C)
+
+        quantize_w(1, 3, 1, w1_last)
+        multiply(1, 3)
+        gb = weave_gated(2, "w1")
+        w3_high = stage.tile([P, PACK * HALF], BF16, name="wb", bufs=4, align_bytes=64)
+        weave("vector", w3_high[:], w_blocks(3, 2, 2))
+        quantize_a(2, 1, d2)
+        quantize_w(2, 0, 3, w2)
+        quantize_a(3, 1, d3)
+        quantize_w(3, 2, 2, w3_high[:])
+        quantize_a(2, 0, gb)
+        second = keep.tile([P, 7 * PACK * P], BF16, name="second", tag="w1", align_bytes=64)
+        w3, g3, w2_last = second[:, 0:1024], second[:, 1024:3072], second[:, 3072:3584]
+        weave("gpsimd", w3, w_blocks(3, 0, 2))
+        nc.gpsimd.tensor_tensor(
+            g3.rearrange("p (c j) -> p c j", j=PACK),
+            picked[3].rearrange("p j c -> p c j"),
+            gates[3][:].unsqueeze(2).to_broadcast([P, C, PACK]),
+            MULT,
+        )
+        weave("gpsimd", w2_last, w_blocks(2, 3, 1))
+        empty(1, 0, False)
+        empty(1, 1, False)
+        scatter_scalar(0, C, C)
+        scatter_scalar(1, C, C)
+        for b in (2, 0, 1):
+            multiply(2, b)
+        empty(1, 3, True)
+        scatter_vector(3, C, C)
+        empty(2, 2, True)
+        scatter_vector(2, 2 * C, C)
+
+        quantize_w(2, 3, 1, w2_last)
+        multiply(2, 3)
+        quantize_w(3, 0, 2, w3)
+        quantize_a(3, 0, g3)
+        empty(2, 0, False)
+        empty(2, 1, False)
+        scatter_scalar(0, 2 * C, C)
+        scatter_scalar(1, 2 * C, C)
+        for b in (2, 0, 3, 1):
+            multiply(3, b)
+        empty(2, 3, True)
+        empty(3, 2, True)
+        scatter_vector(2, 3 * C, C)
+        store(2, nc.sync)
+        empty(3, 3, True)
+        for b in range(2):
+            empty(3, b, False)
+            scatter_scalar(b, 3 * C, C)
+        store(0, nc.sync)
         scatter_vector(3, 2 * C, 2 * C)
-        nc.scalar.dma_start(out[P : 2 * P, :], result[1][:])
-        nc.sync.dma_start(out[3 * P : 4 * P, :], result[3][:])
+        store(1, nc.scalar)
+        store(3, nc.sync)

@@ -4,7 +4,7 @@ import concourse.mybir as mybir
 
 K, T, E, C, N = 512, 2048, 4, 512, 512
 FLOPS = 2 * 2 * N * K * T
-BYTES = 4 * (N * T + (E + 1) * N * K + T + K * T) + 2 * T
+BYTES = 4 * (N * T + (E + 1) * N * K + E * C + K * T) + 2 * 128 * (T // 16)
 
 F32 = mybir.dt.float32
 BF16 = mybir.dt.bfloat16
@@ -14,264 +14,206 @@ U8 = mybir.dt.uint8
 E4M3 = mybir.dt.float8_e4m3fn_x4
 E5M2 = mybir.dt.float8_e5m2_x4
 MULT = mybir.AluOpType.mult
-ADD = mybir.AluOpType.add
 COPY = mybir.ActivationFunctionType.Copy
 
 P = 128
 PACK = 4
 SHARED = E
-KB = K // P
+BLOCKS = K // P
 HALF = K // 2
-PER_COL = 16
-SCALAR_SCATTER = 256
+PER_COLUMN = 16
+RUN = 4
+SCALAR_PIECE = 256
+GATED, PLAIN = 0, 1
+VECTOR_BLOCK = 2
+SPLIT_BLOCK = 3
+SCALAR_EXPERTS = 2
 
 
-def planes_view(t):
-    return t.rearrange("p j (c i) -> p c j i", i=4)
+def planes_view(planes):
+    return planes.rearrange("p j (c i) -> p c j i", i=RUN)
 
 
-def woven_view(t):
-    return t.rearrange("p (c i j) -> p c j i", i=4, j=PACK)
+def woven_view(woven):
+    return woven.rearrange("p (c i j) -> p c j i", i=RUN, j=PACK)
 
 
 def tile_moe_bds_lin_none_kernel(tc, dyT, w, gate, offs, out):
     nc = tc.nc
     with ExitStack() as ctx:
         keep = ctx.enter_context(tc.tile_pool(name="keep", bufs=1))
-        stage = ctx.enter_context(tc.tile_pool(name="stage", bufs=2))
+        stage = ctx.enter_context(tc.tile_pool(name="stage", bufs=1))
         psum = ctx.enter_context(tc.psum_pool(name="psum", bufs=8))
 
-        offsets = keep.tile([P, T // PER_COL], U16, name="offsets")
+        offsets = keep.tile([P, T // PER_COLUMN], U16, name="offsets")
         nc.sync.dma_start(offsets[:], offs)
 
-        def slots(a, n):
-            return offsets[:, a // PER_COL : (a + n) // PER_COL]
+        def entries(first, count):
+            return offsets[:, first // PER_COLUMN : (first + count) // PER_COLUMN]
 
         dy_rows = dyT.rearrange("(p j) t -> p j t", j=PACK)
         dy = [keep.tile([P, T], F32, name="dy%d" % j, tag="row%d" % j) for j in range(PACK)]
+        for j in range(PACK):
+            nc.sync.dma_start(dy[j][:], dy_rows[:, j, :])
+
         gates = [keep.tile([P, C], F32, name="gate%d" % e) for e in range(E)]
         w_raw = {}
-
-        def load_dy(j):
-            nc.sync.dma_start(dy[j][:], dy_rows[:, j, :])
 
         def load_gate(e):
             nc.sync.dma_start(gates[e][:], gate[0:P, e * C : (e + 1) * C])
 
-        def load_w(m, h):
-            t = keep.tile([P, PACK, HALF], F32, name="w%d_%d" % (m, h))
+        def load_w(m, first, width):
+            w_raw[m, first] = keep.tile([P, PACK, width], F32, name="w%d_%d" % (m, first))
             rows = w[m].rearrange("(p j) k -> p j k", j=PACK)
-            nc.sync.dma_start(t[:], rows[:, :, h * HALF : (h + 1) * HALF])
-            w_raw[m, h] = t[:]
+            nc.sync.dma_start(w_raw[m, first][:], rows[:, :, first : first + width])
 
-        def load_w_whole(m):
-            t = keep.tile([P, PACK, K], F32, name="w%d" % m, tag="w%d" % m, align_bytes=64)
-            nc.sync.dma_start(t[:], w[m].rearrange("(p j) k -> p j k", j=PACK))
-            w_raw[m, None] = t[:]
-
-        for j in range(PACK):
-            load_dy(j)
         load_gate(0)
-        for h in range(2):
-            load_w(SHARED, h)
-            load_w(0, h)
+        for first in (0, HALF):
+            load_w(SHARED, first, HALF)
+            load_w(0, first, HALF)
         for e in range(1, E):
             load_gate(e)
-            load_w_whole(e)
+            load_w(e, 0, K)
 
-        pairs = [keep.tile([P, PACK, 2 * C], F32, name="picked%d" % u) for u in range(E // 2)]
+        pairs = [keep.tile([P, PACK, 2 * C], F32, name="pair%d" % u) for u in range(E // 2)]
         picked = [pairs[e // 2][:, :, (e % 2) * C : (e % 2 + 1) * C] for e in range(E)]
-
-        def gather(a, n, j, on_vector):
-            src = dy[j][:].indirect(slots(a, n))
-            u, x = divmod(a, 2 * C)
-            dst = pairs[u][:, j, x : x + n]
-            if on_vector:
-                nc.vector.tensor_copy(dst, src)
-            else:
-                nc.scalar.activation(dst, src, COPY)
-
+        slot_codes = [keep.tile([P, 2 * C], U32, name="slot_codes%d" % e, align_bytes=64) for e in range(E)]
+        slot_scales = [keep.tile([P, 2 * C], U8, name="slot_scales%d" % e, align_bytes=64) for e in range(E)]
+        result = [keep.tile([P, T], F32, name="result%d" % b) for b in range(BLOCKS)]
         w_codes = {}
         w_scales = {}
-        a_codes = [keep.tile([P, 2 * C], U32, name="ac%d" % e, align_bytes=64) for e in range(E)]
-        a_scales = [keep.tile([P, 2 * C], U8, name="as%d" % e, align_bytes=64) for e in range(E)]
-        result = [keep.tile([P, T], F32, name="result%d" % b) for b in range(KB)]
-
-        def weave(engine, dst, src):
-            if engine == "vector":
-                nc.vector.tensor_copy(woven_view(dst), planes_view(src))
-            elif engine == "scalar":
-                nc.scalar.copy(woven_view(dst), planes_view(src))
-            else:
-                nc.gpsimd.tensor_scalar(
-                    dst.rearrange("p (c j) -> p c j", j=PACK), src.rearrange("p j c -> p c j"), 1.0, 0.0, MULT, ADD
-                )
-
-        def weave_w(m, h, engine):
-            wb = stage.tile([P, PACK * HALF], BF16, name="wb", bufs=4, align_bytes=64)
-            weave(engine, wb[:], w_raw[m, h])
-            return wb[:]
-
-        def w_blocks(m, first, count):
-            return w_raw[m, None][:, :, first * P : (first + count) * P]
-
-        def quantize_w(m, first, count, src):
-            codes = keep.tile([P, count * P], U32, name="wc%d_%d" % (m, first), align_bytes=64)
-            scales = keep.tile([P, count * P], U8, name="ws%d_%d" % (m, first), align_bytes=64)
-            nc.vector.quantize_mx(codes[:].bitcast(E4M3), scales[:], src)
-            for x in range(count):
-                w_codes[m, first + x] = codes[:, x * P : (x + 1) * P]
-                w_scales[m, first + x] = scales[:, x * P : (x + 1) * P]
-
-        def weave_gated(e, tag):
-            gb = keep.tile([P, PACK * C], BF16, name="gated%d" % e, tag=tag, align_bytes=64)
-            g = gates[e][:].rearrange("p (c i) -> p c i", i=4).unsqueeze(2).to_broadcast([P, C // 4, PACK, 4])
-            nc.vector.tensor_tensor(woven_view(gb[:]), planes_view(picked[e]), g, MULT)
-            return gb[:]
-
-        def weave_plain(e, engine):
-            db = keep.tile([P, PACK * C], BF16, name="plain%d" % e, tag="plain", align_bytes=64)
-            weave(engine, db[:], picked[e])
-            return db[:]
-
-        def quantize_a(e, s, src):
-            cols = slice(s * C, (s + 1) * C)
-            nc.vector.quantize_mx(a_codes[e][:, cols].bitcast(E5M2), a_scales[e][:, cols], src)
-
         banks = {}
 
+        def gather(first, count, j, on_vector):
+            source = dy[j][:].indirect(entries(first, count))
+            u, x = divmod(first, 2 * C)
+            if on_vector:
+                nc.vector.tensor_copy(pairs[u][:, j, x : x + count], source)
+            else:
+                nc.scalar.activation(pairs[u][:, j, x : x + count], source, COPY)
+
+        def weave(woven, planes, on_vector):
+            copy = nc.vector.tensor_copy if on_vector else nc.scalar.copy
+            copy(woven_view(woven[:]), planes_view(planes))
+            return woven
+
+        def weave_w_half(m, first, on_vector):
+            woven = stage.tile([P, PACK * HALF], BF16, name="w_half", bufs=4, align_bytes=64)
+            return weave(woven, w_raw[m, first][:], on_vector)
+
+        def weave_w(m):
+            woven = stage.tile([P, PACK * K], BF16, name="w_whole", align_bytes=64)
+            return weave(woven, w_raw[m, 0][:], True)
+
+        def weave_plain(e, on_vector):
+            woven = stage.tile([P, PACK * C], BF16, name="plain", align_bytes=64)
+            return weave(woven, picked[e], on_vector)
+
+        def weave_gated(e):
+            woven = stage.tile([P, PACK * C], BF16, name="gated", bufs=2, align_bytes=64)
+            per_slot = gates[e][:].rearrange("p (c i) -> p c i", i=RUN).unsqueeze(2)
+            per_value = per_slot.to_broadcast([P, C // RUN, PACK, RUN])
+            nc.vector.tensor_tensor(woven_view(woven[:]), planes_view(picked[e]), per_value, MULT)
+            return woven
+
+        def quantize_w(m, first, width, woven):
+            codes = keep.tile([P, width], U32, name="w_codes%d_%d" % (m, first), align_bytes=64)
+            scales = keep.tile([P, width], U8, name="w_scales%d_%d" % (m, first), align_bytes=64)
+            nc.vector.quantize_mx(codes[:].bitcast(E4M3), scales[:], woven[:])
+            for x in range(0, width, P):
+                w_codes[m, (first + x) // P] = codes[:, x : x + P]
+                w_scales[m, (first + x) // P] = scales[:, x : x + P]
+
+        def quantize_slots(e, which, woven):
+            cols = slice(which * C, (which + 1) * C)
+            nc.vector.quantize_mx(slot_codes[e][:, cols].bitcast(E5M2), slot_scales[e][:, cols], woven[:])
+
         def multiply(e, b):
-            acc = psum.tile([P, C], F32, name="acc")
-            for s, m in ((1, SHARED), (0, e)):
-                cols = slice(s * C, (s + 1) * C)
+            banks[e, b] = psum.tile([P, C], F32, name="bank")
+            for which, m in ((PLAIN, SHARED), (GATED, e)):
+                cols = slice(which * C, (which + 1) * C)
                 nc.tensor.matmul_mx(
-                    acc[:],
+                    banks[e, b][:],
                     lhsT=w_codes[m, b].bitcast(E4M3),
                     lhsT_scale=w_scales[m, b],
-                    rhs=a_codes[e][:, cols].bitcast(E5M2),
-                    rhs_scale=a_scales[e][:, cols],
-                    start=(s == 1),
-                    stop=(s == 0),
+                    rhs=slot_codes[e][:, cols].bitcast(E5M2),
+                    rhs_scale=slot_scales[e][:, cols],
+                    start=(which == PLAIN),
+                    stop=(which == GATED),
                 )
-            banks[e, b] = acc
 
         def empty(e, b, on_vector):
-            if on_vector:
-                nc.vector.tensor_copy(sums[b][:, e * C : (e + 1) * C], banks[e, b][:])
-            else:
-                nc.scalar.copy(sums[b][:, e * C : (e + 1) * C], banks[e, b][:])
+            copy = nc.vector.tensor_copy if on_vector else nc.scalar.copy
+            copy(sums[b][:, e * C : (e + 1) * C], banks[e, b][:])
+
+        def scatter_scalar(e, blocks):
+            for x in range(e * C, (e + 1) * C, SCALAR_PIECE):
+                for b in blocks:
+                    window = result[b][:].indirect(entries(x, SCALAR_PIECE))
+                    nc.scalar.activation(window, sums[b][:, x : x + SCALAR_PIECE], COPY)
+
+        def scatter_vector(b, first, count):
+            nc.vector.tensor_copy(result[b][:].indirect(entries(first, count)), sums[b][:, first : first + count])
 
         def store(b, queue):
             queue.dma_start(out[b * P : (b + 1) * P, :], result[b][:])
 
-        def scatter_scalar(b, a, n):
-            for x in range(a, a + n, SCALAR_SCATTER):
-                nc.scalar.activation(
-                    result[b][:].indirect(slots(x, SCALAR_SCATTER)), sums[b][:, x : x + SCALAR_SCATTER], COPY
-                )
-
-        def scatter_vector(b, a, n):
-            nc.vector.tensor_copy(result[b][:].indirect(slots(a, n)), sums[b][:, a : a + n])
-
-        for j in range(PACK - 1):
+        last_plane = PACK - 1
+        for j in range(last_plane):
             gather(0, 2 * C, j, True)
             gather(2 * C, 2 * C, j, False)
-        gather(0, C, PACK - 1, True)
-        gather(C, C, PACK - 1, False)
-        db = weave_plain(0, "scalar")
-        gather(2 * C, 2 * C, PACK - 1, False)
-        sums = [keep.tile([P, T], F32, name="sums%d" % b, tag="row%d" % b) for b in range(KB)]
-        gb = weave_gated(0, "gated0")
-        early = [(m, 0, weave_w(m, 0, "vector")) for m in (SHARED, 0)]
-        late = [(m, 1, weave_w(m, 1, "scalar")) for m in (SHARED, 0)]
-        quantize_a(0, 0, gb)
-        quantize_a(0, 1, db)
-        for m, h, wb in early:
-            quantize_w(m, 2 * h, 2, wb)
+        gather(0, C, last_plane, True)
+        gather(C, C, last_plane, False)
+        plain = weave_plain(0, False)
+        gather(2 * C, 2 * C, last_plane, False)
+
+        sums = [keep.tile([P, T], F32, name="sums%d" % b, tag="row%d" % b) for b in range(BLOCKS)]
+
+        gated = weave_gated(0)
+        low = [(m, weave_w_half(m, 0, True)) for m in (SHARED, 0)]
+        high = [(m, weave_w_half(m, HALF, False)) for m in (SHARED, 0)]
+        quantize_slots(0, GATED, gated)
+        quantize_slots(0, PLAIN, plain)
+        for m, woven in low:
+            quantize_w(m, 0, HALF, woven)
         multiply(0, 0)
         multiply(0, 1)
 
-        gb = weave_gated(1, "gated1")
-        for m, h, wb in late:
-            quantize_w(m, 2 * h, 2, wb)
-        multiply(0, 2)
-        multiply(0, 3)
-        db = weave_plain(1, "vector")
-        w1 = keep.tile([P, 3 * PACK * P], BF16, name="w1_woven", align_bytes=64)
-        weave("vector", w1[:], w_blocks(1, 0, 3))
-        quantize_a(1, 1, db)
-        quantize_w(1, 0, 3, w1[:])
-        quantize_a(1, 0, gb)
+        last = E - 1
+        for e in range(last):
+            gated = weave_gated(e + 1)
+            if e == 0:
+                for m, woven in high:
+                    quantize_w(m, HALF, HALF, woven)
+                multiply(0, 2)
+                multiply(0, 3)
+            plain = weave_plain(e + 1, True)
+            weights = weave_w(e + 1)
+            if e > 0:
+                empty(e, VECTOR_BLOCK, True)
+            if e >= SCALAR_EXPERTS:
+                empty(e, SPLIT_BLOCK, True)
+            quantize_slots(e + 1, PLAIN, plain)
+            quantize_w(e + 1, 0, K, weights)
+            quantize_slots(e + 1, GATED, gated)
+            blocks = (0, 1, SPLIT_BLOCK) if e < SCALAR_EXPERTS else (0, 1)
+            for b in blocks:
+                empty(e, b, False)
+            scatter_scalar(e, blocks)
+            if e == 0:
+                empty(0, VECTOR_BLOCK, False)
+            for b in range(BLOCKS) if e + 1 < last else (VECTOR_BLOCK, 0, SPLIT_BLOCK, 1):
+                multiply(e + 1, b)
 
-        first = keep.tile([P, 3 * PACK * C], BF16, name="first", tag="gated1", align_bytes=64)
-        d2, d3 = first[:, 0:2048], first[:, 2048:4096]
-        w2, w1_last = first[:, 4096:5632], first[:, 5632:6144]
-        weave("gpsimd", d2, picked[2])
-        weave("gpsimd", w2, w_blocks(2, 0, 3))
-        weave("gpsimd", d3, picked[3])
-        weave("gpsimd", w1_last, w_blocks(1, 3, 1))
-        empty(0, 0, False)
-        empty(0, 1, False)
-        scatter_scalar(0, 0, C)
-        scatter_scalar(1, 0, C)
-        empty(0, 3, False)
-        scatter_scalar(3, 0, C)
-        for b in (2, 0, 1):
-            multiply(1, b)
-        for e in range(2):
-            empty(e, 2, True)
-            scatter_vector(2, e * C, C)
-
-        quantize_w(1, 3, 1, w1_last)
-        multiply(1, 3)
-        gb = weave_gated(2, "w1")
-        w3_high = stage.tile([P, PACK * HALF], BF16, name="wb", bufs=4, align_bytes=64)
-        weave("vector", w3_high[:], w_blocks(3, 2, 2))
-        quantize_a(2, 1, d2)
-        quantize_w(2, 0, 3, w2)
-        quantize_a(3, 1, d3)
-        quantize_w(3, 2, 2, w3_high[:])
-        quantize_a(2, 0, gb)
-        second = keep.tile([P, 7 * PACK * P], BF16, name="second", tag="w1", align_bytes=64)
-        w3, g3, w2_last = second[:, 0:1024], second[:, 1024:3072], second[:, 3072:3584]
-        weave("gpsimd", w3, w_blocks(3, 0, 2))
-        nc.gpsimd.tensor_tensor(
-            g3.rearrange("p (c j) -> p c j", j=PACK),
-            picked[3].rearrange("p j c -> p c j"),
-            gates[3][:].unsqueeze(2).to_broadcast([P, C, PACK]),
-            MULT,
-        )
-        weave("gpsimd", w2_last, w_blocks(2, 3, 1))
-        empty(1, 0, False)
-        empty(1, 1, False)
-        scatter_scalar(0, C, C)
-        scatter_scalar(1, C, C)
-        for b in (2, 0, 1):
-            multiply(2, b)
-        empty(1, 3, True)
-        scatter_vector(3, C, C)
-        empty(2, 2, True)
-        scatter_vector(2, 2 * C, C)
-
-        quantize_w(2, 3, 1, w2_last)
-        multiply(2, 3)
-        quantize_w(3, 0, 2, w3)
-        quantize_a(3, 0, g3)
-        empty(2, 0, False)
-        empty(2, 1, False)
-        scatter_scalar(0, 2 * C, C)
-        scatter_scalar(1, 2 * C, C)
-        for b in (2, 0, 3, 1):
-            multiply(3, b)
-        empty(2, 3, True)
-        empty(3, 2, True)
-        scatter_vector(2, 3 * C, C)
-        store(2, nc.sync)
-        empty(3, 3, True)
-        for b in range(2):
-            empty(3, b, False)
-            scatter_scalar(b, 3 * C, C)
+        scatter_vector(VECTOR_BLOCK, 0, last * C)
+        empty(last, VECTOR_BLOCK, True)
+        empty(last, SPLIT_BLOCK, True)
+        scatter_vector(VECTOR_BLOCK, last * C, C)
+        store(VECTOR_BLOCK, nc.sync)
+        for b in (0, 1):
+            empty(last, b, False)
+            scatter_scalar(last, (b,))
         store(0, nc.sync)
-        scatter_vector(3, 2 * C, 2 * C)
+        scatter_vector(SPLIT_BLOCK, SCALAR_EXPERTS * C, (E - SCALAR_EXPERTS) * C)
         store(1, nc.scalar)
-        store(3, nc.sync)
+        store(SPLIT_BLOCK, nc.sync)

@@ -97,9 +97,9 @@ def tile_moe_bds_lin_none_kernel(tc, dyT, w, gate, offs, out):
             copy(woven_view(woven[:]), planes_view(planes))
             return woven
 
-        def weave_w_half(m, first, on_vector):
+        def weave_w_half(m, first):
             woven = stage.tile([P, PACK * HALF], BF16, name="w_half", bufs=4, align_bytes=64)
-            return weave(woven, w_raw[m, first][:], on_vector)
+            return weave(woven, w_raw[m, first][:], True)
 
         def weave_w(m):
             woven = stage.tile([P, PACK * K], BF16, name="w_whole", align_bytes=64)
@@ -170,14 +170,14 @@ def tile_moe_bds_lin_none_kernel(tc, dyT, w, gate, offs, out):
         sums = [keep.tile([P, T], F32, name="sums%d" % b, tag="row%d" % b) for b in range(BLOCKS)]
 
         gated = weave_gated(0)
-        low = [(m, weave_w_half(m, 0, True)) for m in (SHARED, 0)]
-        high = [(m, weave_w_half(m, HALF, False)) for m in (SHARED, 0)]
+        low = [(m, weave_w_half(m, 0)) for m in (SHARED, 0)]
         quantize_slots(0, GATED, gated)
-        quantize_slots(0, PLAIN, plain)
         for m, woven in low:
             quantize_w(m, 0, HALF, woven)
+        quantize_slots(0, PLAIN, plain)
         multiply(0, 0)
         multiply(0, 1)
+        high = [(m, weave_w_half(m, HALF)) for m in (SHARED, 0)]
 
         last = E - 1
         for e in range(last):
@@ -189,8 +189,7 @@ def tile_moe_bds_lin_none_kernel(tc, dyT, w, gate, offs, out):
                 multiply(0, 3)
             plain = weave_plain(e + 1, True)
             weights = weave_w(e + 1)
-            if e > 0:
-                empty(e, VECTOR_BLOCK, True)
+            empty(e, VECTOR_BLOCK, True)
             if e >= SCALAR_EXPERTS:
                 empty(e, SPLIT_BLOCK, True)
             quantize_slots(e + 1, PLAIN, plain)
@@ -200,8 +199,6 @@ def tile_moe_bds_lin_none_kernel(tc, dyT, w, gate, offs, out):
             for b in blocks:
                 empty(e, b, False)
             scatter_scalar(e, blocks)
-            if e == 0:
-                empty(0, VECTOR_BLOCK, False)
             for b in range(BLOCKS) if e + 1 < last else (VECTOR_BLOCK, 0, SPLIT_BLOCK, 1):
                 multiply(e + 1, b)
 

from contextlib import ExitStack

import concourse.mybir as mybir

K, T, E, C, N = 512, 2048, 4, 512, 512
FLOPS = 2 * 2 * N * K * T
BYTES = 4 * (N * T + (E + 1) * N * K + E * C + K * T) + 2 * 128 * (T // 16)

F32 = mybir.dt.float32
BF16 = mybir.dt.bfloat16
U32 = mybir.dt.uint32
U16 = mybir.dt.uint16
U8 = mybir.dt.uint8
E4M3 = mybir.dt.float8_e4m3fn_x4
E5M2 = mybir.dt.float8_e5m2_x4
MULT = mybir.AluOpType.mult
COPY = mybir.ActivationFunctionType.Copy

P = 128
PACK = 4
SHARED = E
BLOCKS = K // P
HALF = K // 2
PER_COLUMN = 16
RUN = 4
SCALAR_PIECE = 256
GATED, PLAIN = 0, 1
VECTOR_BLOCK = 2
SPLIT_BLOCK = 3
SCALAR_EXPERTS = 2


def planes_view(planes):
    return planes.rearrange("p j (c i) -> p c j i", i=RUN)


def woven_view(woven):
    return woven.rearrange("p (c i j) -> p c j i", i=RUN, j=PACK)


def tile_moe_bds_lin_none_kernel(tc, dyT, w, gate, offs, out):
    nc = tc.nc
    with ExitStack() as ctx:
        keep = ctx.enter_context(tc.tile_pool(name="keep", bufs=1))
        stage = ctx.enter_context(tc.tile_pool(name="stage", bufs=1))
        psum = ctx.enter_context(tc.psum_pool(name="psum", bufs=8))

        offsets = keep.tile([P, T // PER_COLUMN], U16, name="offsets")
        nc.sync.dma_start(offsets[:], offs)

        def entries(first, count):
            return offsets[:, first // PER_COLUMN : (first + count) // PER_COLUMN]

        dy_rows = dyT.rearrange("(p j) t -> p j t", j=PACK)
        dy = [keep.tile([P, T], F32, name="dy%d" % j, tag="row%d" % j) for j in range(PACK)]
        for j in range(PACK):
            nc.sync.dma_start(dy[j][:], dy_rows[:, j, :])

        gates = [keep.tile([P, C], F32, name="gate%d" % e) for e in range(E)]
        w_raw = {}

        def load_gate(e):
            nc.sync.dma_start(gates[e][:], gate[0:P, e * C : (e + 1) * C])

        def load_w(m, first, width):
            w_raw[m, first] = keep.tile([P, PACK, width], F32, name="w%d_%d" % (m, first))
            rows = w[m].rearrange("(p j) k -> p j k", j=PACK)
            nc.sync.dma_start(w_raw[m, first][:], rows[:, :, first : first + width])

        load_gate(0)
        for first in (0, HALF):
            load_w(SHARED, first, HALF)
            load_w(0, first, HALF)
        for e in range(1, E):
            load_gate(e)
            load_w(e, 0, K)

        pairs = [keep.tile([P, PACK, 2 * C], F32, name="pair%d" % u) for u in range(E // 2)]
        picked = [pairs[e // 2][:, :, (e % 2) * C : (e % 2 + 1) * C] for e in range(E)]
        slot_codes = [keep.tile([P, 2 * C], U32, name="slot_codes%d" % e, align_bytes=64) for e in range(E)]
        slot_scales = [keep.tile([P, 2 * C], U8, name="slot_scales%d" % e, align_bytes=64) for e in range(E)]
        result = [keep.tile([P, T], F32, name="result%d" % b) for b in range(BLOCKS)]
        w_codes = {}
        w_scales = {}
        banks = {}

        def gather(first, count, j, on_vector):
            source = dy[j][:].indirect(entries(first, count))
            u, x = divmod(first, 2 * C)
            if on_vector:
                nc.vector.tensor_copy(pairs[u][:, j, x : x + count], source)
            else:
                nc.scalar.activation(pairs[u][:, j, x : x + count], source, COPY)

        def weave(woven, planes, on_vector):
            copy = nc.vector.tensor_copy if on_vector else nc.scalar.copy
            copy(woven_view(woven[:]), planes_view(planes))
            return woven

        def weave_w_half(m, first):
            woven = stage.tile([P, PACK * HALF], BF16, name="w_half", bufs=4, align_bytes=64)
            return weave(woven, w_raw[m, first][:], True)

        def weave_w(m):
            woven = stage.tile([P, PACK * K], BF16, name="w_whole", align_bytes=64)
            return weave(woven, w_raw[m, 0][:], True)

        def weave_plain(e, on_vector):
            woven = stage.tile([P, PACK * C], BF16, name="plain", align_bytes=64)
            return weave(woven, picked[e], on_vector)

        def weave_gated(e):
            woven = stage.tile([P, PACK * C], BF16, name="gated", bufs=2, align_bytes=64)
            per_slot = gates[e][:].rearrange("p (c i) -> p c i", i=RUN).unsqueeze(2)
            per_value = per_slot.to_broadcast([P, C // RUN, PACK, RUN])
            nc.vector.tensor_tensor(woven_view(woven[:]), planes_view(picked[e]), per_value, MULT)
            return woven

        def quantize_w(m, first, width, woven):
            codes = keep.tile([P, width], U32, name="w_codes%d_%d" % (m, first), align_bytes=64)
            scales = keep.tile([P, width], U8, name="w_scales%d_%d" % (m, first), align_bytes=64)
            nc.vector.quantize_mx(codes[:].bitcast(E4M3), scales[:], woven[:])
            for x in range(0, width, P):
                w_codes[m, (first + x) // P] = codes[:, x : x + P]
                w_scales[m, (first + x) // P] = scales[:, x : x + P]

        def quantize_slots(e, which, woven):
            cols = slice(which * C, (which + 1) * C)
            nc.vector.quantize_mx(slot_codes[e][:, cols].bitcast(E5M2), slot_scales[e][:, cols], woven[:])

        def multiply(e, b):
            banks[e, b] = psum.tile([P, C], F32, name="bank")
            for which, m in ((PLAIN, SHARED), (GATED, e)):
                cols = slice(which * C, (which + 1) * C)
                nc.tensor.matmul_mx(
                    banks[e, b][:],
                    lhsT=w_codes[m, b].bitcast(E4M3),
                    lhsT_scale=w_scales[m, b],
                    rhs=slot_codes[e][:, cols].bitcast(E5M2),
                    rhs_scale=slot_scales[e][:, cols],
                    start=(which == PLAIN),
                    stop=(which == GATED),
                )

        def empty(e, b, on_vector):
            copy = nc.vector.tensor_copy if on_vector else nc.scalar.copy
            copy(sums[b][:, e * C : (e + 1) * C], banks[e, b][:])

        def scatter_scalar(e, blocks):
            for x in range(e * C, (e + 1) * C, SCALAR_PIECE):
                for b in blocks:
                    window = result[b][:].indirect(entries(x, SCALAR_PIECE))
                    nc.scalar.activation(window, sums[b][:, x : x + SCALAR_PIECE], COPY)

        def scatter_vector(b, first, count):
            nc.vector.tensor_copy(result[b][:].indirect(entries(first, count)), sums[b][:, first : first + count])

        def store(b, queue):
            queue.dma_start(out[b * P : (b + 1) * P, :], result[b][:])

        last_plane = PACK - 1
        for j in range(last_plane):
            gather(0, 2 * C, j, True)
            gather(2 * C, 2 * C, j, False)
        gather(0, C, last_plane, True)
        gather(C, C, last_plane, False)
        plain = weave_plain(0, False)
        gather(2 * C, 2 * C, last_plane, False)

        sums = [keep.tile([P, T], F32, name="sums%d" % b, tag="row%d" % b) for b in range(BLOCKS)]

        gated = weave_gated(0)
        low = [(m, weave_w_half(m, 0)) for m in (SHARED, 0)]
        quantize_slots(0, GATED, gated)
        for m, woven in low:
            quantize_w(m, 0, HALF, woven)
        quantize_slots(0, PLAIN, plain)
        multiply(0, 0)
        multiply(0, 1)
        high = [(m, weave_w_half(m, HALF)) for m in (SHARED, 0)]

        last = E - 1
        for e in range(last):
            gated = weave_gated(e + 1)
            if e == 0:
                for m, woven in high:
                    quantize_w(m, HALF, HALF, woven)
                multiply(0, 2)
                multiply(0, 3)
            plain = weave_plain(e + 1, True)
            weights = weave_w(e + 1)
            empty(e, VECTOR_BLOCK, True)
            if e >= SCALAR_EXPERTS:
                empty(e, SPLIT_BLOCK, True)
            quantize_slots(e + 1, PLAIN, plain)
            quantize_w(e + 1, 0, K, weights)
            quantize_slots(e + 1, GATED, gated)
            blocks = (0, 1, SPLIT_BLOCK) if e < SCALAR_EXPERTS else (0, 1)
            for b in blocks:
                empty(e, b, False)
            scatter_scalar(e, blocks)
            for b in range(BLOCKS) if e + 1 < last else (VECTOR_BLOCK, 0, SPLIT_BLOCK, 1):
                multiply(e + 1, b)

        scatter_vector(VECTOR_BLOCK, 0, last * C)
        empty(last, VECTOR_BLOCK, True)
        empty(last, SPLIT_BLOCK, True)
        scatter_vector(VECTOR_BLOCK, last * C, C)
        store(VECTOR_BLOCK, nc.sync)
        for b in (0, 1):
            empty(last, b, False)
            scatter_scalar(last, (b,))
        store(0, nc.sync)
        scatter_vector(SPLIT_BLOCK, SCALAR_EXPERTS * C, (E - SCALAR_EXPERTS) * C)
        store(1, nc.scalar)
        store(SPLIT_BLOCK, nc.sync)
